import numpy as np
import ml_dtypes


def mxq(x, axis, fmt="e4m3"):
    dtype, down = {"e4m3": (ml_dtypes.float8_e4m3fn, 7), "e5m2": (ml_dtypes.float8_e5m2, 14)}[fmt]
    v = np.moveaxis(np.asarray(x, np.float32).astype(ml_dtypes.bfloat16).astype(np.float64), axis, -1)
    blocks = v.reshape(v.shape[:-1] + (-1, 32))
    amax = np.abs(blocks).max(-1, keepdims=True)
    byte = np.maximum(np.where(amax > 0, np.frexp(amax)[1] - 1 + 127, 0) - down, 1)
    scale = np.exp2(byte - 127.0)
    codes = (blocks / scale).astype(np.float32).astype(dtype).astype(np.float64)
    return np.moveaxis((codes * scale).reshape(v.shape), -1, axis)


WIDE = False


def mx_kscale(k):
    if not WIDE:
        return np.ones(k)
    levels = np.array([10, -10, 5, -5, 0])
    if k % 512:
        return np.exp2(np.random.permutation(np.resize(levels, k // 32))).repeat(32)
    a = np.empty((k // 512, 16))
    for p in range(k // 512):
        a[p, :8] = np.random.permutation(np.resize(levels, 8))
        for g in range(8):
            far = levels[np.abs(levels - a[p, g]) >= 10]
            a[p, g + 8] = far[np.random.randint(len(far))]
    return np.exp2(a.ravel()).repeat(32)


def f64(x):
    return np.asarray(x).astype(np.float64)


def striped(idx):
    return np.tile(idx.reshape(-1, 16).T, (8, 1)).astype(np.uint16)


def unstriped(offs):
    return offs[:16].T.reshape(-1).astype(np.int64)


E2M1 = np.array([0.0, 0.5, 1.0, 1.5, 2.0, 3.0, 4.0, 6.0, -0.0, -0.5, -1.0, -1.5, -2.0, -3.0, -4.0, -6.0])


def pack_weight(w, fmt):
    k, n = w.shape
    w = f64(np.asarray(w, np.float32).astype(ml_dtypes.bfloat16)).reshape(k // 32, 32, n)
    amax = np.abs(w).max(1)
    if fmt == "e4m3":
        byte = np.frexp(amax)[1] - 1 + 127 - 7
    else:
        mant, ex = np.frexp(amax / 6.0)
        byte = np.where(mant > 0.5, ex, ex - 1) + 127
    byte = np.clip(np.where(amax > 0, byte, 1), 1, 254)
    scaled = (w * np.exp2(127.0 - byte)[:, None, :]).reshape(k, n).astype(np.float32)
    by_word = np.ascontiguousarray(scaled.reshape(k // 512, 128, 4, n).transpose(0, 1, 3, 2))
    if fmt == "e4m3":
        words = by_word.astype(ml_dtypes.float8_e4m3fn).view(np.uint8)
    else:
        c = by_word.astype(ml_dtypes.float4_e2m1fn).view(np.uint8) & 0xF
        words = (c[..., 0::2] | (c[..., 1::2] << 4)).reshape(k // 512, 128, 2 * n)
    return np.ascontiguousarray(words), np.ascontiguousarray(byte.astype(np.uint8).reshape(k // 512, 16, n))


def unpack_weight(words, scales, fmt):
    g, _, n = scales.shape
    words = np.ascontiguousarray(words).reshape(g, 128, n, -1)
    if fmt == "e4m3":
        vals = words.view(ml_dtypes.float8_e4m3fn).astype(np.float64)
    else:
        nib = np.empty((g, 128, n, 4), np.uint8)
        nib[..., 0::2] = words & 0xF
        nib[..., 1::2] = words >> 4
        vals = E2M1[nib]
    vals = vals * np.repeat(np.exp2(scales.astype(np.float64) - 127.0), 8, axis=1)[..., None]
    return vals.transpose(0, 1, 3, 2).reshape(g * 512, n)


def gelu(v):
    return 0.5 * v * (1.0 + np.tanh(np.sqrt(2.0 / np.pi) * (v + 0.044715 * v**3)))


K, T, S, H, T3, S2, P = 1536, 4096, 1024, 512, 2048, 1024, 512


def setup_inputs():
    n = np.random.standard_normal
    s = mx_kscale(K)[:, None]
    u = mx_kscale(H)[:, None]
    d = {}
    d["tab_words"], d["tab_scales"] = pack_weight(n((K, T)) * s, "e4m3")
    d["offs"] = striped(np.random.permutation(T)[:S])
    d["tab2_words"], d["tab2_scales"] = pack_weight(n((H, T3)) / u / H**0.5, "e4m3")
    d["offs2"] = striped(np.random.permutation(T3)[:S2])
    d["pos1"] = striped(np.random.permutation(S)[:P])
    d["pos2"] = striped(np.random.permutation(S)[:P])
    d["w1"] = (1.5 * n((K, H)) / s / K**0.5).astype(np.float32)
    d["w4_words"], d["w4_scales"] = pack_weight(1.5 * n((K, H)) / s / K**0.5, "e2m1")
    d["gain"] = (0.8 * np.exp(0.4 * n(H)) * u[:, 0]).astype(np.float32)
    d["hint"] = np.random.uniform(0.5, 3.5, S2).astype(np.float32)
    return d


def reference(tab_words, tab_scales, offs, tab2_words, tab2_scales, offs2, pos1, pos2,
              w1, w4_words, w4_scales, gain, hint):
    v = unpack_weight(tab_words, tab_scales, "e4m3")[:, unstriped(offs)]
    v2 = unpack_weight(tab2_words, tab2_scales, "e4m3")[:, unstriped(offs2)]
    s = mxq(f64(w1), 0, "e4m3").T @ v
    b = unpack_weight(w4_words, w4_scales, "e2m1").T @ v
    h = f64(gain)[:, None] * np.maximum(s, np.tanh(s) * b)
    e = v2.T @ mxq(h, 0, "e4m3")
    stuck = e[:, unstriped(pos1)]
    solving = e[:, unstriped(pos2)]
    return np.square(stuck) - f64(hint)[:, None] * solving

@@ -1,0 +1,278 @@
+from contextlib import ExitStack
+
+import concourse.mybir as mybir
+
+K, T, S, H, T3, S2, NP = 1536, 4096, 1024, 512, 2048, 1024, 512
+FLOPS = 2 * (2 * K * H * S + H * S2 * S)
+
+F32 = mybir.dt.float32
+BF16 = mybir.dt.bfloat16
+I32 = mybir.dt.int32
+U32 = mybir.dt.uint32
+U16 = mybir.dt.uint16
+U8 = mybir.dt.uint8
+FP8X4 = mybir.dt.float8_e4m3fn_x4
+FP4X4 = mybir.dt.float4_e2m1fn_x4
+ACT = mybir.ActivationFunctionType
+ALU = mybir.AluOpType
+
+P = 128
+PACK = 4
+PASSES = K // (P * PACK)
+BANK = 512
+HALVES = S // BANK
+CARD_SLICE = 512
+CAST_ON_VECTOR = 80
+WEAVE_ON_VECTOR = 320
+
+
+def tile_list_hint_card_bench_kernel(
+    tc, tab_words, tab_scales, offs, tab2_words, tab2_scales, offs2, pos1, pos2,
+    w1, w4_words, w4_scales, gain, hint, out,
+):
+    nc = tc.nc
+    with ExitStack() as ctx:
+        keep = ctx.enter_context(tc.tile_pool(name="keep", bufs=1))
+        ring = ctx.enter_context(tc.tile_pool(name="ring", bufs=2))
+        psum = ctx.enter_context(tc.psum_pool(name="psum", bufs=1))
+
+        def held(shape, dtype, name):
+            return keep.tile(shape, dtype, name=name, align_bytes=64)
+
+        def bank(index):
+            return psum.tile([P, BANK], F32, name="bank%d" % index, tag="bank%d" % index)
+
+        offs_sb = keep.tile([P, S // 16], U16, name="offs_sb")
+        offs2_sb = keep.tile([P, S2 // 16], U16, name="offs2_sb")
+        pos1_sb = keep.tile([P, NP // 16], U16, name="pos1_sb")
+        pos2_sb = keep.tile([P, NP // 16], U16, name="pos2_sb")
+
+        v_table = [held([P, T], I32, "v_table%d" % a) for a in range(PASSES)]
+        v_scale_table = held([P, T], U8, "v_scale_table")
+        v_scale = [held([P, S], U8, "v_scale%d" % a) for a in range(PASSES)]
+        v_words = [[held([P, BANK], U32, "v_words%d_%d" % (a, c)) for c in range(HALVES)] for a in range(PASSES)]
+        w1_raw = [held([P, PACK, H], F32, "w1_raw%d" % a) for a in range(PASSES)]
+        w1_words = [held([P, H], U32, "w1_words%d" % a) for a in range(PASSES)]
+        w1_scale = [held([P, H], U8, "w1_scale%d" % a) for a in range(PASSES)]
+        w4_raw = held([P, PASSES, 2 * H], U8, "w4_raw")
+        w4_scale_raw = held([P, PASSES, H], U8, "w4_scale_raw")
+        w4_dealt = [held([P, 2 * H], U8, "w4_dealt%d" % a) for a in range(PASSES)]
+        w4_scale = [held([P, H], U8, "w4_scale%d" % a) for a in range(PASSES)]
+        card_table = held([P, T3], I32, "card_table")
+        card_scale_table = held([P, T3], U8, "card_scale_table")
+        slices = S2 // CARD_SLICE
+        card_words = [held([P, CARD_SLICE], U32, "card_words%d" % c) for c in range(slices)]
+        card_scale = [held([P, CARD_SLICE], U8, "card_scale%d" % c) for c in range(slices)]
+        gain_sb = held([P, PACK], F32, "gain_sb")
+        hint_sb = held([P, S2 // P], F32, "hint_sb")
+        minus_hint = held([P, S2 // P], F32, "minus_hint")
+        h_words = [held([P, BANK], U32, "h_words%d" % c) for c in range(HALVES)]
+        h_scale = [held([P, BANK], U8, "h_scale%d" % c) for c in range(HALVES)]
+
+        nc.vector.memset(v_scale_table[:].bitcast(I32), 0)
+        nc.vector.memset(card_scale_table[:].bitcast(I32), 0)
+        nc.vector.memset(w4_scale_raw[:].rearrange("p a c -> p (a c)").bitcast(I32), 0)
+        for a in range(1, PASSES):
+            nc.vector.memset(v_scale[a][:].bitcast(I32), 0)
+        for q in range(4):
+            nc.gpsimd.dma_start(
+                out=v_scale_table[32 * q : 32 * q + 4 * PASSES, :].bitcast(I32),
+                in_=tab_scales[:, 4 * q : 4 * q + 4, :].bitcast(I32),
+            )
+        for q in range(4):
+            nc.gpsimd.dma_start(
+                out=w4_scale_raw[32 * q : 32 * q + 4].bitcast(I32),
+                in_=w4_scales[:, 4 * q : 4 * q + 4, :].rearrange("a r c -> r a c").bitcast(I32),
+            )
+
+        nc.sync.dma_start(offs2_sb[:], offs2)
+        nc.sync.dma_start(out=card_table[:], in_=tab2_words[0].rearrange("p t i -> p (t i)").bitcast(I32))
+        nc.sync.dma_start(offs_sb[:], offs)
+
+        def load_table(a):
+            nc.sync.dma_start(out=v_table[a][:], in_=tab_words[a].rearrange("p t i -> p (t i)").bitcast(I32))
+
+        def load_w1(a):
+            rows = w1[a * P * PACK : (a + 1) * P * PACK, :]
+            nc.sync.dma_start(out=w1_raw[a][:], in_=rows.rearrange("(p i) r -> p i r", i=PACK))
+
+        nc.sync.dma_start(out=w4_raw[:].bitcast(I32), in_=w4_words.rearrange("a p c -> p a c").bitcast(I32))
+        load_table(0)
+        for q in range(4):
+            nc.sync.dma_start(
+                out=card_scale_table[32 * q : 32 * q + 4, :].bitcast(I32),
+                in_=tab2_scales[0, 4 * q : 4 * q + 4, :].bitcast(I32),
+            )
+        load_w1(0)
+        for a in range(1, PASSES):
+            load_table(a)
+            load_w1(a)
+        nc.sync.dma_start(out=gain_sb[:], in_=gain.rearrange("(p t) -> p t", t=PACK))
+        nc.sync.dma_start(pos1_sb[:], pos1)
+        nc.sync.dma_start(pos2_sb[:], pos2)
+        with nc.allow_non_contiguous_dma(reason="one hint factor to each partition"):
+            nc.sync.dma_start(out=hint_sb[:], in_=hint.rearrange("(c p) -> p c", p=P))
+        nc.gpsimd.tensor_scalar(minus_hint[:], hint_sb[:], -1.0, 0.0, ALU.mult, ALU.add)
+
+        nc.vector.tensor_copy(v_scale[0][:], v_scale_table[:].indirect(offs_sb[:]))
+        for a in range(1, PASSES):
+            nc.gpsimd.dma_start(
+                out=v_scale[a][0 : P - 4 * a, :].bitcast(I32), in_=v_scale[0][4 * a : P, :].bitcast(I32)
+            )
+
+        def gather_words(a, c):
+            columns = slice(c * BANK // 16, (c + 1) * BANK // 16)
+            nc.vector.tensor_copy(v_words[a][c][:], v_table[a][:].bitcast(U32).indirect(offs_sb[:, columns]))
+
+        def deal_w4(a):
+            nc.vector.tensor_copy(
+                w4_dealt[a][:].rearrange("p (t m e) -> p t m e", t=PACK, e=2),
+                w4_raw[:, a, :].rearrange("p (m t e) -> p t m e", t=PACK, e=2),
+            )
+            nc.vector.tensor_copy(
+                w4_scale[a][:].rearrange("p (t m) -> p t m", t=PACK),
+                w4_scale_raw[:, a, :].rearrange("p (m t) -> p t m", t=PACK),
+            )
+
+        def quantize_w1(a):
+            grouped = ring.tile([P, PACK * H], BF16, name="w1_grouped", align_bytes=64)
+            dst = grouped[:].rearrange("p (t m i) -> p m i t", t=PACK, i=PACK)
+            src = w1_raw[a][:].rearrange("p i (m t) -> p m i t", t=PACK)
+            if a < PASSES - 1:
+                nc.scalar.activation(dst, src, ACT.Copy)
+                nc.vector.quantize_mx(w1_words[a][:].bitcast(FP8X4), w1_scale[a][:], grouped[:])
+            else:
+                nc.vector.tensor_copy(dst[:, :CAST_ON_VECTOR], src[:, :CAST_ON_VECTOR])
+                nc.scalar.activation(dst[:, CAST_ON_VECTOR:], src[:, CAST_ON_VECTOR:], ACT.Copy)
+                for t in range(PACK):
+                    cols = slice(t * P, (t + 1) * P)
+                    nc.vector.quantize_mx(
+                        w1_words[a][:, cols].bitcast(FP8X4), w1_scale[a][:, cols],
+                        grouped[:, t * H : (t + 1) * H],
+                    )
+
+        def b_pass(acc, a, c, t):
+            nc.tensor.matmul_mx(
+                acc[:],
+                lhsT=w4_dealt[a][:, 2 * t * P : 2 * (t + 1) * P].bitcast(FP4X4),
+                lhsT_scale=w4_scale[a][:, t * P : (t + 1) * P],
+                rhs=v_words[a][c][:].bitcast(FP8X4),
+                rhs_scale=v_scale[a][:, c * BANK : (c + 1) * BANK],
+                start=(a == 0), stop=(a == PASSES - 1),
+            )
+
+        def s_pass(acc, a, c, t):
+            nc.tensor.matmul_mx(
+                acc[:],
+                lhsT=w1_words[a][:, t * P : (t + 1) * P].bitcast(FP8X4),
+                lhsT_scale=w1_scale[a][:, t * P : (t + 1) * P],
+                rhs=v_words[a][c][:].bitcast(FP8X4),
+                rhs_scale=v_scale[a][:, c * BANK : (c + 1) * BANK],
+                start=(a == 0), stop=(a == PASSES - 1),
+            )
+
+        def modulate(s_acc, b_acc):
+            th = ring.tile([P, BANK], F32, name="th")
+            nc.scalar.activation(th[:], s_acc[:], ACT.Tanh)
+            tb = ring.tile([P, BANK], F32, name="tb")
+            nc.vector.tensor_tensor(tb[:], b_acc[:], th[:], ALU.mult)
+            return tb
+
+        def make_h_rows(s_acc, tb, c, t):
+            top = ring.tile([P, BANK], F32, name="top")
+            nc.vector.tensor_tensor(top[:], s_acc[:], tb[:], ALU.max)
+            nc.scalar.activation(planes[c][:, t, :], top[:], ACT.Copy, scale=gain_sb[:, t : t + 1])
+
+        def weave(copy, c, first, last):
+            copy(
+                woven[c][:, first * PACK : last * PACK].rearrange("p (c i t) -> p c t i", i=4, t=PACK),
+                planes[c][:, :, first:last].rearrange("p t (c i) -> p c t i", i=4),
+            )
+
+        def quantize_h(c):
+            nc.vector.quantize_mx(h_words[c][:].bitcast(FP8X4), h_scale[c][:], woven[c][:])
+
+        planes = [held([P, PACK, BANK], BF16, "h_planes%d" % c) for c in range(HALVES)]
+        woven = [held([P, BANK * PACK], BF16, "h_woven%d" % c) for c in range(HALVES)]
+
+        for c in range(slices):
+            columns = slice(c * CARD_SLICE // 16, (c + 1) * CARD_SLICE // 16)
+            nc.vector.tensor_copy(card_words[c][:], card_table[:].bitcast(U32).indirect(offs2_sb[:, columns]))
+            nc.vector.tensor_copy(card_scale[c][:], card_scale_table[:].indirect(offs2_sb[:, columns]))
+
+        s_banks = [bank(2 * t) for t in range(PACK)]
+        b_banks = [bank(2 * t + 1) for t in range(PACK)]
+        for a in range(PASSES):
+            gather_words(a, 0)
+            if a == 0:
+                for x in range(PASSES):
+                    deal_w4(x)
+            for t in range(PACK):
+                b_pass(b_banks[t], a, 0, t)
+            gather_words(a, 1)
+            quantize_w1(a)
+            for t in range(PACK):
+                s_pass(s_banks[t], a, 0, t)
+
+        waiting = None
+        for t in range(PACK):
+            tb = modulate(s_banks[t], b_banks[t])
+            if waiting is not None:
+                make_h_rows(*waiting)
+            waiting = (s_banks[t], tb, 0, t)
+        make_h_rows(*waiting)
+        for t in range(PACK):
+            s_acc = bank(2 * t + 1)
+            for a in range(PASSES):
+                s_pass(s_acc, a, 1, t)
+            b_acc = bank(2 * t)
+            for a in range(PASSES):
+                b_pass(b_acc, a, 1, t)
+            make_h_rows(s_acc, modulate(s_acc, b_acc), 1, t)
+            if t < PACK - 1:
+                weave(nc.scalar.copy, 0, (0, 160, 336)[t], (160, 336, 512)[t])
+            if t == PACK - 2:
+                quantize_h(0)
+        weave(nc.vector.tensor_copy, 1, 0, WEAVE_ON_VECTOR)
+        weave(nc.scalar.copy, 1, WEAVE_ON_VECTOR, BANK)
+        quantize_h(1)
+
+        def finish(m, square, solving, first, last):
+            result = ring.tile([P, last - first], F32, name="result", bufs=3)
+            nc.vector.scalar_tensor_tensor(
+                result[:], solving[:], minus_hint[:, m : m + 1], square[:, first:last], ALU.mult, ALU.add
+            )
+            nc.sync.dma_start(out=out[m * P : (m + 1) * P, first:last], in_=result[:])
+
+        def pick_solving(scores, first, last):
+            solving = ring.tile([P, last - first], F32, name="solving", bufs=3)
+            nc.vector.tensor_copy(solving[:], scores[:].indirect(pos2_sb[:, first // 16 : last // 16]))
+            return solving
+
+        waiting = None
+        for m in range(S2 // P):
+            scores = ring.tile([P, S], F32, name="scores", bufs=3)
+            part, first = divmod(m * P, CARD_SLICE)
+            for c in range(HALVES):
+                acc = bank(7 if c == 0 else m % 7)
+                nc.tensor.matmul_mx(
+                    acc[:],
+                    lhsT=card_words[part][:, first : first + P].bitcast(FP8X4),
+                    lhsT_scale=card_scale[part][:, first : first + P],
+                    rhs=h_words[c][:].bitcast(FP8X4),
+                    rhs_scale=h_scale[c][:],
+                    start=True, stop=True,
+                )
+                nc.scalar.copy(scores[:, c * BANK : (c + 1) * BANK], acc[:])
+            stuck = ring.tile([P, NP], F32, name="stuck")
+            nc.vector.tensor_copy(stuck[:], scores[:].indirect(pos1_sb[:]))
+            square = ring.tile([P, NP], F32, name="square")
+            nc.scalar.activation(square[:], stuck[:], ACT.Square)
+            if waiting is not None:
+                finish(*waiting)
+            if m < S2 // P - 1:
+                waiting = (m, square, pick_solving(scores, 0, NP), 0, NP)
+        pieces = [(first, first + NP // 2) for first in (0, NP // 2)]
+        picked = [pick_solving(scores, first, last) for first, last in pieces]
+        for solving, (first, last) in zip(picked, pieces):
+            finish(m, square, solving, first, last)

@@ -21,8 +21,7 @@ PACK = 4
 PASSES = K // (P * PACK)
 BANK = 512
 HALVES = S // BANK
-CARD_SLICE = 512
-CAST_ON_VECTOR = 80
+FIRST_CARDS = 384
 WEAVE_ON_VECTOR = 320
 
 
@@ -49,6 +48,7 @@ def tile_list_hint_card_bench_kernel(
 
         v_table = [held([P, T], I32, "v_table%d" % a) for a in range(PASSES)]
         v_scale_table = held([P, T], U8, "v_scale_table")
+        v_scale_rows = held([P, S], U8, "v_scale_rows")
         v_scale = [held([P, S], U8, "v_scale%d" % a) for a in range(PASSES)]
         v_words = [[held([P, BANK], U32, "v_words%d_%d" % (a, c)) for c in range(HALVES)] for a in range(PASSES)]
         w1_raw = [held([P, PACK, H], F32, "w1_raw%d" % a) for a in range(PASSES)]
@@ -60,65 +60,66 @@ def tile_list_hint_card_bench_kernel(
         w4_scale = [held([P, H], U8, "w4_scale%d" % a) for a in range(PASSES)]
         card_table = held([P, T3], I32, "card_table")
         card_scale_table = held([P, T3], U8, "card_scale_table")
-        slices = S2 // CARD_SLICE
-        card_words = [held([P, CARD_SLICE], U32, "card_words%d" % c) for c in range(slices)]
-        card_scale = [held([P, CARD_SLICE], U8, "card_scale%d" % c) for c in range(slices)]
+        card_scale = held([P, S2], U8, "card_scale")
         gain_sb = held([P, PACK], F32, "gain_sb")
         hint_sb = held([P, S2 // P], F32, "hint_sb")
         minus_hint = held([P, S2 // P], F32, "minus_hint")
         h_words = [held([P, BANK], U32, "h_words%d" % c) for c in range(HALVES)]
         h_scale = [held([P, BANK], U8, "h_scale%d" % c) for c in range(HALVES)]
 
-        nc.vector.memset(v_scale_table[:].bitcast(I32), 0)
-        nc.vector.memset(card_scale_table[:].bitcast(I32), 0)
-        nc.vector.memset(w4_scale_raw[:].rearrange("p a c -> p (a c)").bitcast(I32), 0)
-        for a in range(1, PASSES):
+        nc.gpsimd.memset(v_scale_table[64:80, :].bitcast(I32), 0)
+        for first in (0, 96):
+            nc.vector.memset(v_scale_table[first : first + 32, :].bitcast(I32), 0)
+        for a in range(PASSES):
             nc.vector.memset(v_scale[a][:].bitcast(I32), 0)
-        for q in range(4):
-            nc.gpsimd.dma_start(
-                out=v_scale_table[32 * q : 32 * q + 4 * PASSES, :].bitcast(I32),
-                in_=tab_scales[:, 4 * q : 4 * q + 4, :].bitcast(I32),
-            )
-        for q in range(4):
-            nc.gpsimd.dma_start(
-                out=w4_scale_raw[32 * q : 32 * q + 4].bitcast(I32),
-                in_=w4_scales[:, 4 * q : 4 * q + 4, :].rearrange("a r c -> r a c").bitcast(I32),
-            )
+        nc.gpsimd.memset(w4_scale_raw[:].rearrange("p a c -> p (a c)").bitcast(I32), 0)
+        nc.gpsimd.memset(card_scale_table[:].bitcast(I32), 0)
 
-        nc.sync.dma_start(offs2_sb[:], offs2)
-        nc.sync.dma_start(out=card_table[:], in_=tab2_words[0].rearrange("p t i -> p (t i)").bitcast(I32))
-        nc.sync.dma_start(offs_sb[:], offs)
+        def table_half(a, half):
+            columns = slice(half * T // 2, (half + 1) * T // 2)
+            words = tab_words[a].rearrange("p t i -> p (t i)").bitcast(I32)
+            return v_table[a][:, columns], words[:, columns]
 
-        def load_table(a):
-            nc.sync.dma_start(out=v_table[a][:], in_=tab_words[a].rearrange("p t i -> p (t i)").bitcast(I32))
-
-        def load_w1(a):
+        def w1_rows(a):
             rows = w1[a * P * PACK : (a + 1) * P * PACK, :]
-            nc.sync.dma_start(out=w1_raw[a][:], in_=rows.rearrange("(p i) r -> p i r", i=PACK))
+            return w1_raw[a][:], rows.rearrange("(p i) r -> p i r", i=PACK)
 
+        nc.sync.dma_start(offs_sb[:], offs)
+        scale_rows = tab_scales.rearrange("a q t -> (a q) t").bitcast(I32)
+        nc.sync.dma_start(out=v_scale_table[32:64, :].bitcast(I32), in_=scale_rows[0:32, :])
+        nc.sync.dma_start(out=v_scale_table[80:96, :].bitcast(I32), in_=scale_rows[32:48, :])
+        nc.vector.tensor_copy(v_scale_rows[:], v_scale_table[:].indirect(offs_sb[:]))
         nc.sync.dma_start(out=w4_raw[:].bitcast(I32), in_=w4_words.rearrange("a p c -> p a c").bitcast(I32))
-        load_table(0)
+        nc.sync.dma_start(offs2_sb[:], offs2)
+
+        large = [
+            table_half(0, 0), table_half(0, 1), w1_rows(0), table_half(1, 0), table_half(1, 1),
+            w1_rows(2), w1_rows(1), table_half(2, 0), table_half(2, 1),
+        ]
+        small = []
         for q in range(4):
-            nc.sync.dma_start(
-                out=card_scale_table[32 * q : 32 * q + 4, :].bitcast(I32),
-                in_=tab2_scales[0, 4 * q : 4 * q + 4, :].bitcast(I32),
-            )
-        load_w1(0)
-        for a in range(1, PASSES):
-            load_table(a)
-            load_w1(a)
+            rows = w4_scales[:, 4 * q : 4 * q + 4, :].rearrange("a r c -> r a c")
+            small.append((w4_scale_raw[32 * q : 32 * q + 4], rows))
+        for q in range(4):
+            small.append((card_scale_table[32 * q + 4 : 32 * q + 8, :], tab2_scales[0, 4 * q : 4 * q + 4, :]))
+        for a in range(PASSES):
+            for q in range(4):
+                first = (32, 48, 80)[a] + 4 * q
+                small.append((v_scale[a][32 * q : 32 * q + 4, :], v_scale_rows[first : first + 4, :]))
+        sent = 0
+        for n, (dst, src) in enumerate(large):
+            nc.sync.dma_start(out=dst, in_=src)
+            count = 3 - n % 2
+            for small_dst, small_src in small[sent : sent + count]:
+                nc.sync.dma_start(out=small_dst.bitcast(I32), in_=small_src.bitcast(I32))
+            sent = sent + count
         nc.sync.dma_start(out=gain_sb[:], in_=gain.rearrange("(p t) -> p t", t=PACK))
+        nc.sync.dma_start(out=card_table[:], in_=tab2_words[0].rearrange("p t i -> p (t i)").bitcast(I32))
         nc.sync.dma_start(pos1_sb[:], pos1)
         nc.sync.dma_start(pos2_sb[:], pos2)
         with nc.allow_non_contiguous_dma(reason="one hint factor to each partition"):
             nc.sync.dma_start(out=hint_sb[:], in_=hint.rearrange("(c p) -> p c", p=P))
         nc.gpsimd.tensor_scalar(minus_hint[:], hint_sb[:], -1.0, 0.0, ALU.mult, ALU.add)
-
-        nc.vector.tensor_copy(v_scale[0][:], v_scale_table[:].indirect(offs_sb[:]))
-        for a in range(1, PASSES):
-            nc.gpsimd.dma_start(
-                out=v_scale[a][0 : P - 4 * a, :].bitcast(I32), in_=v_scale[0][4 * a : P, :].bitcast(I32)
-            )
 
         def gather_words(a, c):
             columns = slice(c * BANK // 16, (c + 1) * BANK // 16)
@@ -126,8 +127,8 @@ def tile_list_hint_card_bench_kernel(
 
         def deal_w4(a):
             nc.vector.tensor_copy(
-                w4_dealt[a][:].rearrange("p (t m e) -> p t m e", t=PACK, e=2),
-                w4_raw[:, a, :].rearrange("p (m t e) -> p t m e", t=PACK, e=2),
+                w4_dealt[a][:].bitcast(U16).rearrange("p (t m) -> p t m", t=PACK),
+                w4_raw[:, a, :].bitcast(U16).rearrange("p (m t) -> p t m", t=PACK),
             )
             nc.vector.tensor_copy(
                 w4_scale[a][:].rearrange("p (t m) -> p t m", t=PACK),
@@ -138,18 +139,8 @@ def tile_list_hint_card_bench_kernel(
             grouped = ring.tile([P, PACK * H], BF16, name="w1_grouped", align_bytes=64)
             dst = grouped[:].rearrange("p (t m i) -> p m i t", t=PACK, i=PACK)
             src = w1_raw[a][:].rearrange("p i (m t) -> p m i t", t=PACK)
-            if a < PASSES - 1:
-                nc.scalar.activation(dst, src, ACT.Copy)
-                nc.vector.quantize_mx(w1_words[a][:].bitcast(FP8X4), w1_scale[a][:], grouped[:])
-            else:
-                nc.vector.tensor_copy(dst[:, :CAST_ON_VECTOR], src[:, :CAST_ON_VECTOR])
-                nc.scalar.activation(dst[:, CAST_ON_VECTOR:], src[:, CAST_ON_VECTOR:], ACT.Copy)
-                for t in range(PACK):
-                    cols = slice(t * P, (t + 1) * P)
-                    nc.vector.quantize_mx(
-                        w1_words[a][:, cols].bitcast(FP8X4), w1_scale[a][:, cols],
-                        grouped[:, t * H : (t + 1) * H],
-                    )
+            nc.scalar.activation(dst, src, ACT.Copy)
+            nc.vector.quantize_mx(w1_words[a][:].bitcast(FP8X4), w1_scale[a][:], grouped[:])
 
         def b_pass(acc, a, c, t):
             nc.tensor.matmul_mx(
@@ -171,10 +162,9 @@ def tile_list_hint_card_bench_kernel(
                 start=(a == 0), stop=(a == PASSES - 1),
             )
 
-        def modulate(s_acc, b_acc):
+        def modulate(s_acc, b_acc, tb):
             th = ring.tile([P, BANK], F32, name="th")
             nc.scalar.activation(th[:], s_acc[:], ACT.Tanh)
-            tb = ring.tile([P, BANK], F32, name="tb")
             nc.vector.tensor_tensor(tb[:], b_acc[:], th[:], ALU.mult)
             return tb
 
@@ -195,47 +185,59 @@ def tile_list_hint_card_bench_kernel(
         planes = [held([P, PACK, BANK], BF16, "h_planes%d" % c) for c in range(HALVES)]
         woven = [held([P, BANK * PACK], BF16, "h_woven%d" % c) for c in range(HALVES)]
 
-        for c in range(slices):
-            columns = slice(c * CARD_SLICE // 16, (c + 1) * CARD_SLICE // 16)
-            nc.vector.tensor_copy(card_words[c][:], card_table[:].bitcast(U32).indirect(offs2_sb[:, columns]))
-            nc.vector.tensor_copy(card_scale[c][:], card_scale_table[:].indirect(offs2_sb[:, columns]))
+        nc.vector.tensor_copy(card_scale[:], card_scale_table[:].indirect(offs2_sb[:]))
 
         s_banks = [bank(2 * t) for t in range(PACK)]
         b_banks = [bank(2 * t + 1) for t in range(PACK)]
         for a in range(PASSES):
+            deal_w4(a)
+        for a in range(PASSES - 1):
             gather_words(a, 0)
-            if a == 0:
-                for x in range(PASSES):
-                    deal_w4(x)
             for t in range(PACK):
                 b_pass(b_banks[t], a, 0, t)
             gather_words(a, 1)
+            if a == 1:
+                quantize_w1(2)
             quantize_w1(a)
             for t in range(PACK):
                 s_pass(s_banks[t], a, 0, t)
+        gather_words(PASSES - 1, 0)
+        gather_words(PASSES - 1, 1)
+        for t in range(PACK):
+            s_pass(s_banks[t], PASSES - 1, 0, t)
+            b_pass(b_banks[t], PASSES - 1, 0, t)
 
         waiting = None
-        for t in range(PACK):
-            tb = modulate(s_banks[t], b_banks[t])
-            if waiting is not None:
-                make_h_rows(*waiting)
-            waiting = (s_banks[t], tb, 0, t)
+        for c in range(HALVES):
+            for t in range(PACK):
+                if c == 0:
+                    s_acc, b_acc = s_banks[t], b_banks[t]
+                else:
+                    s_acc = bank(2 * t + 1)
+                    for a in range(PASSES):
+                        s_pass(s_acc, a, c, t)
+                    b_acc = bank(2 * t)
+                    for a in range(PASSES):
+                        b_pass(b_acc, a, c, t)
+                tb = modulate(s_acc, b_acc, held([P, BANK], F32, "tb%d" % (t % 2)))
+                if waiting is not None:
+                    make_h_rows(*waiting)
+                waiting = (s_acc, tb, c, t)
+                if (c, t) == (1, 0):
+                    nc.gpsimd.tensor_scalar(
+                        woven[0][:].rearrange("p (j t) -> p j t", t=PACK), planes[0][:].rearrange("p t j -> p j t"),
+                        1.0, 0.0, ALU.mult, ALU.add,
+                    )
+                if (c, t) == (1, 2):
+                    quantize_h(0)
         make_h_rows(*waiting)
-        for t in range(PACK):
-            s_acc = bank(2 * t + 1)
-            for a in range(PASSES):
-                s_pass(s_acc, a, 1, t)
-            b_acc = bank(2 * t)
-            for a in range(PASSES):
-                b_pass(b_acc, a, 1, t)
-            make_h_rows(s_acc, modulate(s_acc, b_acc), 1, t)
-            if t < PACK - 1:
-                weave(nc.scalar.copy, 0, (0, 160, 336)[t], (160, 336, 512)[t])
-            if t == PACK - 2:
-                quantize_h(0)
+        early_cards = keep.tile([P, FIRST_CARDS], U32, name="early_cards", tag="tb1", align_bytes=64)
+        nc.vector.tensor_copy(early_cards[:], card_table[:].bitcast(U32).indirect(offs2_sb[:, : FIRST_CARDS // 16]))
         weave(nc.vector.tensor_copy, 1, 0, WEAVE_ON_VECTOR)
         weave(nc.scalar.copy, 1, WEAVE_ON_VECTOR, BANK)
         quantize_h(1)
+        late_cards = keep.tile([P, S2 - FIRST_CARDS], U32, name="late_cards", tag="h_woven1", align_bytes=64)
+        nc.vector.tensor_copy(late_cards[:], card_table[:].bitcast(U32).indirect(offs2_sb[:, FIRST_CARDS // 16 :]))
 
         def finish(m, square, solving, first, last):
             result = ring.tile([P, last - first], F32, name="result", bufs=3)
@@ -249,29 +251,48 @@ def tile_list_hint_card_bench_kernel(
             nc.vector.tensor_copy(solving[:], scores[:].indirect(pos2_sb[:, first // 16 : last // 16]))
             return solving
 
-        waiting = None
-        for m in range(S2 // P):
-            scores = ring.tile([P, S], F32, name="scores", bufs=3)
-            part, first = divmod(m * P, CARD_SLICE)
+        def finish_on_gpsimd(m, square, solving):
+            scaled = ring.tile([P, NP], F32, name="scaled")
+            nc.gpsimd.tensor_scalar(scaled[:], solving[:], minus_hint[:, m : m + 1], 0.0, ALU.mult, ALU.add)
+            result = ring.tile([P, NP], F32, name="result", bufs=3)
+            nc.gpsimd.tensor_tensor(result[:], scaled[:], square[:], ALU.add)
+            nc.sync.dma_start(out=out[m * P : (m + 1) * P, :], in_=result[:])
+
+        def make_scores(m):
+            if m == 0:
+                scores = keep.tile([P, S], F32, name="first_scores", tag="h_planes1", align_bytes=64)
+            else:
+                scores = ring.tile([P, S], F32, name="scores", bufs=3)
+            first = m * P
+            if first < FIRST_CARDS:
+                cards = early_cards[:, first : first + P]
+            else:
+                cards = late_cards[:, first - FIRST_CARDS : first - FIRST_CARDS + P]
             for c in range(HALVES):
                 acc = bank(7 if c == 0 else m % 7)
                 nc.tensor.matmul_mx(
                     acc[:],
-                    lhsT=card_words[part][:, first : first + P].bitcast(FP8X4),
-                    lhsT_scale=card_scale[part][:, first : first + P],
+                    lhsT=cards.bitcast(FP8X4),
+                    lhsT_scale=card_scale[4:P, first : first + P],
                     rhs=h_words[c][:].bitcast(FP8X4),
                     rhs_scale=h_scale[c][:],
                     start=True, stop=True,
                 )
                 nc.scalar.copy(scores[:, c * BANK : (c + 1) * BANK], acc[:])
+            return scores
+
+        tiles = S2 // P
+        ahead = make_scores(0)
+        for m in range(tiles):
+            scores = ahead
+            if m + 1 < tiles:
+                ahead = make_scores(m + 1)
             stuck = ring.tile([P, NP], F32, name="stuck")
             nc.vector.tensor_copy(stuck[:], scores[:].indirect(pos1_sb[:]))
             square = ring.tile([P, NP], F32, name="square")
             nc.scalar.activation(square[:], stuck[:], ACT.Square)
-            if waiting is not None:
-                finish(*waiting)
-            if m < S2 // P - 1:
-                waiting = (m, square, pick_solving(scores, 0, NP), 0, NP)
+            if m + 1 < tiles:
+                finish_on_gpsimd(m, square, pick_solving(scores, 0, NP))
         pieces = [(first, first + NP // 2) for first in (0, NP // 2)]
         picked = [pick_solving(scores, first, last) for first, last in pieces]
         for solving, (first, last) in zip(picked, pieces):

from contextlib import ExitStack

import concourse.mybir as mybir

K, T, S, H, T3, S2, NP = 1536, 4096, 1024, 512, 2048, 1024, 512
FLOPS = 2 * (2 * K * H * S + H * S2 * S)

F32 = mybir.dt.float32
BF16 = mybir.dt.bfloat16
I32 = mybir.dt.int32
U32 = mybir.dt.uint32
U16 = mybir.dt.uint16
U8 = mybir.dt.uint8
FP8X4 = mybir.dt.float8_e4m3fn_x4
FP4X4 = mybir.dt.float4_e2m1fn_x4
ACT = mybir.ActivationFunctionType
ALU = mybir.AluOpType

P = 128
PACK = 4
PASSES = K // (P * PACK)
BANK = 512
HALVES = S // BANK
FIRST_CARDS = 384
WEAVE_ON_VECTOR = 320


def tile_list_hint_card_bench_kernel(
    tc, tab_words, tab_scales, offs, tab2_words, tab2_scales, offs2, pos1, pos2,
    w1, w4_words, w4_scales, gain, hint, out,
):
    nc = tc.nc
    with ExitStack() as ctx:
        keep = ctx.enter_context(tc.tile_pool(name="keep", bufs=1))
        ring = ctx.enter_context(tc.tile_pool(name="ring", bufs=2))
        psum = ctx.enter_context(tc.psum_pool(name="psum", bufs=1))

        def held(shape, dtype, name):
            return keep.tile(shape, dtype, name=name, align_bytes=64)

        def bank(index):
            return psum.tile([P, BANK], F32, name="bank%d" % index, tag="bank%d" % index)

        offs_sb = keep.tile([P, S // 16], U16, name="offs_sb")
        offs2_sb = keep.tile([P, S2 // 16], U16, name="offs2_sb")
        pos1_sb = keep.tile([P, NP // 16], U16, name="pos1_sb")
        pos2_sb = keep.tile([P, NP // 16], U16, name="pos2_sb")

        v_table = [held([P, T], I32, "v_table%d" % a) for a in range(PASSES)]
        v_scale_table = held([P, T], U8, "v_scale_table")
        v_scale_rows = held([P, S], U8, "v_scale_rows")
        v_scale = [held([P, S], U8, "v_scale%d" % a) for a in range(PASSES)]
        v_words = [[held([P, BANK], U32, "v_words%d_%d" % (a, c)) for c in range(HALVES)] for a in range(PASSES)]
        w1_raw = [held([P, PACK, H], F32, "w1_raw%d" % a) for a in range(PASSES)]
        w1_words = [held([P, H], U32, "w1_words%d" % a) for a in range(PASSES)]
        w1_scale = [held([P, H], U8, "w1_scale%d" % a) for a in range(PASSES)]
        w4_raw = held([P, PASSES, 2 * H], U8, "w4_raw")
        w4_scale_raw = held([P, PASSES, H], U8, "w4_scale_raw")
        w4_dealt = [held([P, 2 * H], U8, "w4_dealt%d" % a) for a in range(PASSES)]
        w4_scale = [held([P, H], U8, "w4_scale%d" % a) for a in range(PASSES)]
        card_table = held([P, T3], I32, "card_table")
        card_scale_table = held([P, T3], U8, "card_scale_table")
        card_scale = held([P, S2], U8, "card_scale")
        gain_sb = held([P, PACK], F32, "gain_sb")
        hint_sb = held([P, S2 // P], F32, "hint_sb")
        minus_hint = held([P, S2 // P], F32, "minus_hint")
        h_words = [held([P, BANK], U32, "h_words%d" % c) for c in range(HALVES)]
        h_scale = [held([P, BANK], U8, "h_scale%d" % c) for c in range(HALVES)]

        nc.gpsimd.memset(v_scale_table[64:80, :].bitcast(I32), 0)
        for first in (0, 96):
            nc.vector.memset(v_scale_table[first : first + 32, :].bitcast(I32), 0)
        for a in range(PASSES):
            nc.vector.memset(v_scale[a][:].bitcast(I32), 0)
        nc.gpsimd.memset(w4_scale_raw[:].rearrange("p a c -> p (a c)").bitcast(I32), 0)
        nc.gpsimd.memset(card_scale_table[:].bitcast(I32), 0)

        def table_half(a, half):
            columns = slice(half * T // 2, (half + 1) * T // 2)
            words = tab_words[a].rearrange("p t i -> p (t i)").bitcast(I32)
            return v_table[a][:, columns], words[:, columns]

        def w1_rows(a):
            rows = w1[a * P * PACK : (a + 1) * P * PACK, :]
            return w1_raw[a][:], rows.rearrange("(p i) r -> p i r", i=PACK)

        nc.sync.dma_start(offs_sb[:], offs)
        scale_rows = tab_scales.rearrange("a q t -> (a q) t").bitcast(I32)
        nc.sync.dma_start(out=v_scale_table[32:64, :].bitcast(I32), in_=scale_rows[0:32, :])
        nc.sync.dma_start(out=v_scale_table[80:96, :].bitcast(I32), in_=scale_rows[32:48, :])
        nc.vector.tensor_copy(v_scale_rows[:], v_scale_table[:].indirect(offs_sb[:]))
        nc.sync.dma_start(out=w4_raw[:].bitcast(I32), in_=w4_words.rearrange("a p c -> p a c").bitcast(I32))
        nc.sync.dma_start(offs2_sb[:], offs2)

        large = [
            table_half(0, 0), table_half(0, 1), w1_rows(0), table_half(1, 0), table_half(1, 1),
            w1_rows(2), w1_rows(1), table_half(2, 0), table_half(2, 1),
        ]
        small = []
        for q in range(4):
            rows = w4_scales[:, 4 * q : 4 * q + 4, :].rearrange("a r c -> r a c")
            small.append((w4_scale_raw[32 * q : 32 * q + 4], rows))
        for q in range(4):
            small.append((card_scale_table[32 * q + 4 : 32 * q + 8, :], tab2_scales[0, 4 * q : 4 * q + 4, :]))
        for a in range(PASSES):
            for q in range(4):
                first = (32, 48, 80)[a] + 4 * q
                small.append((v_scale[a][32 * q : 32 * q + 4, :], v_scale_rows[first : first + 4, :]))
        sent = 0
        for n, (dst, src) in enumerate(large):
            nc.sync.dma_start(out=dst, in_=src)
            count = 3 - n % 2
            for small_dst, small_src in small[sent : sent + count]:
                nc.sync.dma_start(out=small_dst.bitcast(I32), in_=small_src.bitcast(I32))
            sent = sent + count
        nc.sync.dma_start(out=gain_sb[:], in_=gain.rearrange("(p t) -> p t", t=PACK))
        nc.sync.dma_start(out=card_table[:], in_=tab2_words[0].rearrange("p t i -> p (t i)").bitcast(I32))
        nc.sync.dma_start(pos1_sb[:], pos1)
        nc.sync.dma_start(pos2_sb[:], pos2)
        with nc.allow_non_contiguous_dma(reason="one hint factor to each partition"):
            nc.sync.dma_start(out=hint_sb[:], in_=hint.rearrange("(c p) -> p c", p=P))
        nc.gpsimd.tensor_scalar(minus_hint[:], hint_sb[:], -1.0, 0.0, ALU.mult, ALU.add)

        def gather_words(a, c):
            columns = slice(c * BANK // 16, (c + 1) * BANK // 16)
            nc.vector.tensor_copy(v_words[a][c][:], v_table[a][:].bitcast(U32).indirect(offs_sb[:, columns]))

        def deal_w4(a):
            nc.vector.tensor_copy(
                w4_dealt[a][:].bitcast(U16).rearrange("p (t m) -> p t m", t=PACK),
                w4_raw[:, a, :].bitcast(U16).rearrange("p (m t) -> p t m", t=PACK),
            )
            nc.vector.tensor_copy(
                w4_scale[a][:].rearrange("p (t m) -> p t m", t=PACK),
                w4_scale_raw[:, a, :].rearrange("p (m t) -> p t m", t=PACK),
            )

        def quantize_w1(a):
            grouped = ring.tile([P, PACK * H], BF16, name="w1_grouped", align_bytes=64)
            dst = grouped[:].rearrange("p (t m i) -> p m i t", t=PACK, i=PACK)
            src = w1_raw[a][:].rearrange("p i (m t) -> p m i t", t=PACK)
            nc.scalar.activation(dst, src, ACT.Copy)
            nc.vector.quantize_mx(w1_words[a][:].bitcast(FP8X4), w1_scale[a][:], grouped[:])

        def b_pass(acc, a, c, t):
            nc.tensor.matmul_mx(
                acc[:],
                lhsT=w4_dealt[a][:, 2 * t * P : 2 * (t + 1) * P].bitcast(FP4X4),
                lhsT_scale=w4_scale[a][:, t * P : (t + 1) * P],
                rhs=v_words[a][c][:].bitcast(FP8X4),
                rhs_scale=v_scale[a][:, c * BANK : (c + 1) * BANK],
                start=(a == 0), stop=(a == PASSES - 1),
            )

        def s_pass(acc, a, c, t):
            nc.tensor.matmul_mx(
                acc[:],
                lhsT=w1_words[a][:, t * P : (t + 1) * P].bitcast(FP8X4),
                lhsT_scale=w1_scale[a][:, t * P : (t + 1) * P],
                rhs=v_words[a][c][:].bitcast(FP8X4),
                rhs_scale=v_scale[a][:, c * BANK : (c + 1) * BANK],
                start=(a == 0), stop=(a == PASSES - 1),
            )

        def modulate(s_acc, b_acc, tb):
            th = ring.tile([P, BANK], F32, name="th")
            nc.scalar.activation(th[:], s_acc[:], ACT.Tanh)
            nc.vector.tensor_tensor(tb[:], b_acc[:], th[:], ALU.mult)
            return tb

        def make_h_rows(s_acc, tb, c, t):
            top = ring.tile([P, BANK], F32, name="top")
            nc.vector.tensor_tensor(top[:], s_acc[:], tb[:], ALU.max)
            nc.scalar.activation(planes[c][:, t, :], top[:], ACT.Copy, scale=gain_sb[:, t : t + 1])

        def weave(copy, c, first, last):
            copy(
                woven[c][:, first * PACK : last * PACK].rearrange("p (c i t) -> p c t i", i=4, t=PACK),
                planes[c][:, :, first:last].rearrange("p t (c i) -> p c t i", i=4),
            )

        def quantize_h(c):
            nc.vector.quantize_mx(h_words[c][:].bitcast(FP8X4), h_scale[c][:], woven[c][:])

        planes = [held([P, PACK, BANK], BF16, "h_planes%d" % c) for c in range(HALVES)]
        woven = [held([P, BANK * PACK], BF16, "h_woven%d" % c) for c in range(HALVES)]

        nc.vector.tensor_copy(card_scale[:], card_scale_table[:].indirect(offs2_sb[:]))

        s_banks = [bank(2 * t) for t in range(PACK)]
        b_banks = [bank(2 * t + 1) for t in range(PACK)]
        for a in range(PASSES):
            deal_w4(a)
        for a in range(PASSES - 1):
            gather_words(a, 0)
            for t in range(PACK):
                b_pass(b_banks[t], a, 0, t)
            gather_words(a, 1)
            if a == 1:
                quantize_w1(2)
            quantize_w1(a)
            for t in range(PACK):
                s_pass(s_banks[t], a, 0, t)
        gather_words(PASSES - 1, 0)
        gather_words(PASSES - 1, 1)
        for t in range(PACK):
            s_pass(s_banks[t], PASSES - 1, 0, t)
            b_pass(b_banks[t], PASSES - 1, 0, t)

        waiting = None
        for c in range(HALVES):
            for t in range(PACK):
                if c == 0:
                    s_acc, b_acc = s_banks[t], b_banks[t]
                else:
                    s_acc = bank(2 * t + 1)
                    for a in range(PASSES):
                        s_pass(s_acc, a, c, t)
                    b_acc = bank(2 * t)
                    for a in range(PASSES):
                        b_pass(b_acc, a, c, t)
                tb = modulate(s_acc, b_acc, held([P, BANK], F32, "tb%d" % (t % 2)))
                if waiting is not None:
                    make_h_rows(*waiting)
                waiting = (s_acc, tb, c, t)
                if (c, t) == (1, 0):
                    nc.gpsimd.tensor_scalar(
                        woven[0][:].rearrange("p (j t) -> p j t", t=PACK), planes[0][:].rearrange("p t j -> p j t"),
                        1.0, 0.0, ALU.mult, ALU.add,
                    )
                if (c, t) == (1, 2):
                    quantize_h(0)
        make_h_rows(*waiting)
        early_cards = keep.tile([P, FIRST_CARDS], U32, name="early_cards", tag="tb1", align_bytes=64)
        nc.vector.tensor_copy(early_cards[:], card_table[:].bitcast(U32).indirect(offs2_sb[:, : FIRST_CARDS // 16]))
        weave(nc.vector.tensor_copy, 1, 0, WEAVE_ON_VECTOR)
        weave(nc.scalar.copy, 1, WEAVE_ON_VECTOR, BANK)
        quantize_h(1)
        late_cards = keep.tile([P, S2 - FIRST_CARDS], U32, name="late_cards", tag="h_woven1", align_bytes=64)
        nc.vector.tensor_copy(late_cards[:], card_table[:].bitcast(U32).indirect(offs2_sb[:, FIRST_CARDS // 16 :]))

        def finish(m, square, solving, first, last):
            result = ring.tile([P, last - first], F32, name="result", bufs=3)
            nc.vector.scalar_tensor_tensor(
                result[:], solving[:], minus_hint[:, m : m + 1], square[:, first:last], ALU.mult, ALU.add
            )
            nc.sync.dma_start(out=out[m * P : (m + 1) * P, first:last], in_=result[:])

        def pick_solving(scores, first, last):
            solving = ring.tile([P, last - first], F32, name="solving", bufs=3)
            nc.vector.tensor_copy(solving[:], scores[:].indirect(pos2_sb[:, first // 16 : last // 16]))
            return solving

        def finish_on_gpsimd(m, square, solving):
            scaled = ring.tile([P, NP], F32, name="scaled")
            nc.gpsimd.tensor_scalar(scaled[:], solving[:], minus_hint[:, m : m + 1], 0.0, ALU.mult, ALU.add)
            result = ring.tile([P, NP], F32, name="result", bufs=3)
            nc.gpsimd.tensor_tensor(result[:], scaled[:], square[:], ALU.add)
            nc.sync.dma_start(out=out[m * P : (m + 1) * P, :], in_=result[:])

        def make_scores(m):
            if m == 0:
                scores = keep.tile([P, S], F32, name="first_scores", tag="h_planes1", align_bytes=64)
            else:
                scores = ring.tile([P, S], F32, name="scores", bufs=3)
            first = m * P
            if first < FIRST_CARDS:
                cards = early_cards[:, first : first + P]
            else:
                cards = late_cards[:, first - FIRST_CARDS : first - FIRST_CARDS + P]
            for c in range(HALVES):
                acc = bank(7 if c == 0 else m % 7)
                nc.tensor.matmul_mx(
                    acc[:],
                    lhsT=cards.bitcast(FP8X4),
                    lhsT_scale=card_scale[4:P, first : first + P],
                    rhs=h_words[c][:].bitcast(FP8X4),
                    rhs_scale=h_scale[c][:],
                    start=True, stop=True,
                )
                nc.scalar.copy(scores[:, c * BANK : (c + 1) * BANK], acc[:])
            return scores

        tiles = S2 // P
        ahead = make_scores(0)
        for m in range(tiles):
            scores = ahead
            if m + 1 < tiles:
                ahead = make_scores(m + 1)
            stuck = ring.tile([P, NP], F32, name="stuck")
            nc.vector.tensor_copy(stuck[:], scores[:].indirect(pos1_sb[:]))
            square = ring.tile([P, NP], F32, name="square")
            nc.scalar.activation(square[:], stuck[:], ACT.Square)
            if m + 1 < tiles:
                finish_on_gpsimd(m, square, pick_solving(scores, 0, NP))
        pieces = [(first, first + NP // 2) for first in (0, NP // 2)]
        picked = [pick_solving(scores, first, last) for first, last in pieces]
        for solving, (first, last) in zip(picked, pieces):
            finish(m, square, solving, first, last)
